import numpy as np
import ml_dtypes


def mxq(x, axis, fmt="e4m3"):
    dtype, down = {"e4m3": (ml_dtypes.float8_e4m3fn, 7), "e5m2": (ml_dtypes.float8_e5m2, 14)}[fmt]
    v = np.moveaxis(np.asarray(x, np.float32).astype(ml_dtypes.bfloat16).astype(np.float64), axis, -1)
    blocks = v.reshape(v.shape[:-1] + (-1, 32))
    amax = np.abs(blocks).max(-1, keepdims=True)
    byte = np.maximum(np.where(amax > 0, np.frexp(amax)[1] - 1 + 127, 0) - down, 1)
    scale = np.exp2(byte - 127.0)
    codes = (blocks / scale).astype(np.float32).astype(dtype).astype(np.float64)
    return np.moveaxis((codes * scale).reshape(v.shape), -1, axis)


WIDE = False


def mx_kscale(k):
    if not WIDE:
        return np.ones(k)
    levels = np.array([10, -10, 5, -5, 0])
    if k % 512:
        return np.exp2(np.random.permutation(np.resize(levels, k // 32))).repeat(32)
    a = np.empty((k // 512, 16))
    for p in range(k // 512):
        a[p, :8] = np.random.permutation(np.resize(levels, 8))
        for g in range(8):
            far = levels[np.abs(levels - a[p, g]) >= 10]
            a[p, g + 8] = far[np.random.randint(len(far))]
    return np.exp2(a.ravel()).repeat(32)


def f64(x):
    return np.asarray(x).astype(np.float64)


def striped(idx):
    return np.tile(idx.reshape(-1, 16).T, (8, 1)).astype(np.uint16)


def unstriped(offs):
    return offs[:16].T.reshape(-1).astype(np.int64)


K, T, D, S, V, N = 1024, 1024, 8, 4096, 512, 128


def setup_inputs():
    n = np.random.standard_normal
    s = mx_kscale(K)[:, None]
    return {
        "xT": (n((K, T)) * s).astype(np.float32),
        "w": (n((K, N)) / np.sqrt(K) / s).astype(np.float32),
        "b": (0.3 * n((N, 1))).astype(np.float32),
        "gate": np.tile(np.random.uniform(0.2, 1.0, (D, 1, V)) / np.sqrt(D), (1, N, 1)).astype(np.float32),
        "pos1": striped(np.random.permutation(T)[:V]),
        "pos2": striped(np.random.permutation(T)[:V]),
        "pos3": striped(np.random.permutation(T)[:V]),
        "pos4": striped(np.random.permutation(T)[:V]),
        "pos5": striped(np.random.permutation(T)[:V]),
        "pos6": striped(np.random.permutation(T)[:V]),
        "pos7": striped(np.random.permutation(T)[:V]),
        "pos8": striped(np.random.permutation(T)[:V]),
    }


def reference(xT, w, b, gate, pos1, pos2, pos3, pos4, pos5, pos6, pos7, pos8):
    y = mxq(f64(w), 0, "e4m3").T @ mxq(f64(xT), 0, "e4m3")
    y = y + f64(b)
    return sum(f64(gate[d]) * y[:, unstriped(p)] for d, p in enumerate((pos1, pos2, pos3, pos4, pos5, pos6, pos7, pos8)))

@@ -1,0 +1,153 @@
+from contextlib import ExitStack
+
+import concourse.mybir as mybir
+from concourse.masks import make_identity
+
+K, T, D, V, M = 1024, 1024, 8, 512, 128
+P = 128
+PACK = 4
+K_PASS = P * PACK
+PASSES = K // K_PASS
+
+FLOPS = 2 * K * T * M + 2 * D * V * M
+
+F32 = mybir.dt.float32
+BF16 = mybir.dt.bfloat16
+U32 = mybir.dt.uint32
+U16 = mybir.dt.uint16
+U8 = mybir.dt.uint8
+FP8X4 = mybir.dt.float8_e4m3fn_x4
+MULT = mybir.AluOpType.mult
+ADD = mybir.AluOpType.add
+IDENTITY = mybir.ActivationFunctionType.Identity
+
+
+RANGES = ((0, 512), (512, 256), (768, 256))
+LOADS = ((0, 0, 512), (0, 512, 512), (1, 0, 512), (1, 512, 256), (1, 768, 256))
+
+
+def tile_picked_agg_lin_bias_sub_l_kernel(
+    tc, xT, w, b, gate, pos1, pos2, pos3, pos4, pos5, pos6, pos7, pos8, out
+):
+    nc = tc.nc
+    lists = (pos1, pos2, pos3, pos4, pos5, pos6, pos7, pos8)
+    with ExitStack() as ctx:
+        keep = ctx.enter_context(tc.tile_pool(name="keep", bufs=1))
+        psum = ctx.enter_context(tc.psum_pool(name="psum", bufs=1))
+
+        bias = keep.tile([P, 1], F32, name="bias")
+        nc.scalar.dma_start(out=bias[:], in_=b)
+        ident = keep.tile([P, P], F32, name="ident")
+        make_identity(nc, ident[:])
+
+        w_raw = keep.tile([P, PASSES, PACK, M], F32, name="w_raw")
+        nc.sync.dma_start(out=w_raw[:], in_=w.rearrange("(c p j) m -> p c j m", c=PASSES, j=PACK))
+        raws = {}
+        for c, t0, n in LOADS:
+            raw = keep.tile([P, PACK, n], F32, name=f"raw{c}_{t0}")
+            nc.sync.dma_start(
+                out=raw[:],
+                in_=xT[c * K_PASS : (c + 1) * K_PASS, t0 : t0 + n].rearrange("(p j) w -> p j w", j=PACK),
+            )
+            raws[(c, t0)] = raw
+        offs = []
+        gates = []
+        for d in range(D):
+            off = keep.tile([P, V // 16], U16, name=f"off{d}")
+            nc.sync.dma_start(off[:], lists[d])
+            offs.append(off)
+            g = keep.tile([P, V], F32, name=f"gate{d}")
+            nc.sync.dma_start(out=g[:], in_=gate[d])
+            gates.append(g)
+
+        w_grp = keep.tile([P, PASSES, M, PACK], BF16, name="w_grp", align_bytes=64)
+        w_codes = keep.tile([P, PASSES * M], U32, name="w_codes", align_bytes=64)
+        w_scales = keep.tile([P, PASSES * M], U8, name="w_scales", align_bytes=64)
+        nc.vector.tensor_copy(out=w_grp[:, 0], in_=w_raw[:, 0].rearrange("p j m -> p m j"))
+        nc.scalar.copy(out=w_grp[:, 1], in_=w_raw[:, 1].rearrange("p j m -> p m j"))
+        nc.vector.quantize_mx(
+            out=w_codes[:].bitcast(FP8X4), scales=w_scales[:], in_=w_grp[:].rearrange("p c m j -> p (c m j)")
+        )
+
+        y = keep.tile([P, T], F32, name="y")
+        x_codes = keep.tile([P, PASSES, T], U32, name="x_codes", align_bytes=64)
+        x_scales = keep.tile([P, PASSES, T], U8, name="x_scales", align_bytes=64)
+        banks = {}
+        for t0, n in RANGES:
+            bank = psum.tile([P, n], F32, name=f"y{t0}")
+            banks[t0] = bank
+
+        for c, t0, n in LOADS:
+            raw = raws[(c, t0)]
+            grp = keep.tile([P, n, PACK], BF16, name=f"grp{c}_{t0}", align_bytes=64)
+            cut = n * 5 // 8
+            nc.scalar.copy(out=grp[:, cut:], in_=raw[:, :, cut:].rearrange("p j w -> p w j"))
+            nc.vector.tensor_copy(out=grp[:, :cut], in_=raw[:, :, :cut].rearrange("p j w -> p w j"))
+            nc.vector.quantize_mx(
+                out=x_codes[:, c, t0 : t0 + n].bitcast(FP8X4),
+                scales=x_scales[:, c, t0 : t0 + n],
+                in_=grp[:].rearrange("p w j -> p (w j)"),
+            )
+            for r0, rn in RANGES:
+                if t0 <= r0 < t0 + n:
+                    nc.tensor.matmul_mx(
+                        out=banks[r0][:],
+                        lhsT=w_codes[:, c * M : (c + 1) * M].bitcast(FP8X4),
+                        lhsT_scale=w_scales[:, c * M : (c + 1) * M],
+                        rhs=x_codes[:, c, r0 : r0 + rn].bitcast(FP8X4),
+                        rhs_scale=x_scales[:, c, r0 : r0 + rn],
+                        start=(c == 0),
+                        stop=(c == PASSES - 1),
+                    )
+                    if c == PASSES - 1:
+                        nc.scalar.activation(
+                            out=y[:, r0 : r0 + rn], in_=banks[r0][:], func=IDENTITY, bias=bias[:]
+                        )
+
+        H = V // 2
+        prods = []
+        accs = []
+        for d in range(D):
+            prod = keep.tile([P, V], F32, name=f"prod{d}")
+            prods.append(prod)
+        for i in range(V // P):
+            acc = psum.tile([P, P], F32, name=f"acc{i}")
+            accs.append(acc)
+        back = [psum.tile([P, H], F32, name=f"back{h}", tag=("back0", "y0")[h]) for h in range(2)]
+        turned = keep.tile([P, V], F32, name="turned")
+        res = keep.tile([P, V], F32, name="res")
+
+        def gather(d, lo, hi):
+            nc.vector.tensor_tensor(
+                prods[d][:, lo:hi], y[:].indirect(offs[d][:, lo // 16 : hi // 16]), gates[d][:, lo:hi], MULT
+            )
+
+        def add_up(d, lo, hi, last):
+            for i in range(lo // P, hi // P):
+                nc.tensor.matmul(
+                    accs[i][:], prods[d][:, i * P : (i + 1) * P], ident[:], start=(d == 0), stop=(d == last), is_transpose=True
+                )
+
+        def turn_back(h):
+            for i in range(2 * h, 2 * h + 2):
+                nc.scalar.copy(out=turned[:, i * P : (i + 1) * P], in_=accs[i][:])
+                nc.tensor.transpose(back[h][:, (i - 2 * h) * P : (i - 2 * h + 1) * P], turned[:, i * P : (i + 1) * P], ident[:])
+
+        for d in range(6):
+            gather(d, 0, V)
+            add_up(d, 0, H, 7)
+            add_up(d, H, V, 5)
+        gather(6, 0, H)
+        add_up(6, 0, H, 7)
+        gather(7, 0, H)
+        turn_back(1)
+        add_up(7, 0, H, 7)
+        gather(6, H, V)
+        gather(7, H, V)
+        turn_back(0)
+        nc.scalar.copy(out=res[:, :H], in_=back[0][:])
+        nc.sync.dma_start(out=out[:, :H], in_=res[:, :H])
+        pair = keep.tile([P, H], F32, name="pair")
+        nc.vector.tensor_tensor(pair[:], prods[6][:, H:], prods[7][:, H:], ADD)
+        nc.vector.tensor_tensor(res[:, H:], pair[:], back[1][:], ADD)
+        nc.sync.dma_start(out=out[:, H:], in_=res[:, H:])

@@ -22,8 +22,9 @@ ADD = mybir.AluOpType.add
 IDENTITY = mybir.ActivationFunctionType.Identity
 
 
-RANGES = ((0, 512), (512, 256), (768, 256))
 LOADS = ((0, 0, 512), (0, 512, 512), (1, 0, 512), (1, 512, 256), (1, 768, 256))
+RANGES = ((0, 512), (512, 256), (768, 256))
+UNITS = ((0, 0, 512, 8), (0, 512, 512, 8), (1, 0, 512, 8), (1, 512, 256, 8), (1, 768, 256, 12))
 
 
 def tile_picked_agg_lin_bias_sub_l_kernel(
@@ -35,21 +36,21 @@ def tile_picked_agg_lin_bias_sub_l_kernel(
         keep = ctx.enter_context(tc.tile_pool(name="keep", bufs=1))
         psum = ctx.enter_context(tc.psum_pool(name="psum", bufs=1))
 
-        bias = keep.tile([P, 1], F32, name="bias")
-        nc.scalar.dma_start(out=bias[:], in_=b)
         ident = keep.tile([P, P], F32, name="ident")
         make_identity(nc, ident[:])
 
         w_raw = keep.tile([P, PASSES, PACK, M], F32, name="w_raw")
         nc.sync.dma_start(out=w_raw[:], in_=w.rearrange("(c p j) m -> p c j m", c=PASSES, j=PACK))
-        raws = {}
+        raws = []
         for c, t0, n in LOADS:
             raw = keep.tile([P, PACK, n], F32, name=f"raw{c}_{t0}")
             nc.sync.dma_start(
                 out=raw[:],
                 in_=xT[c * K_PASS : (c + 1) * K_PASS, t0 : t0 + n].rearrange("(p j) w -> p j w", j=PACK),
             )
-            raws[(c, t0)] = raw
+            raws.append((c, t0, n, raw))
+        bias = keep.tile([P, 1], F32, name="bias")
+        nc.sync.dma_start(out=bias[:], in_=b)
         offs = []
         gates = []
         for d in range(D):
@@ -60,11 +61,17 @@ def tile_picked_agg_lin_bias_sub_l_kernel(
             nc.sync.dma_start(out=g[:], in_=gate[d])
             gates.append(g)
 
+        def interleave(copy, grouped, raw):
+            copy(
+                out=grouped.rearrange("p (g i) j -> p g j i", i=4),
+                in_=raw.rearrange("p j (g i) -> p g j i", i=4),
+            )
+
         w_grp = keep.tile([P, PASSES, M, PACK], BF16, name="w_grp", align_bytes=64)
         w_codes = keep.tile([P, PASSES * M], U32, name="w_codes", align_bytes=64)
         w_scales = keep.tile([P, PASSES * M], U8, name="w_scales", align_bytes=64)
-        nc.vector.tensor_copy(out=w_grp[:, 0], in_=w_raw[:, 0].rearrange("p j m -> p m j"))
-        nc.scalar.copy(out=w_grp[:, 1], in_=w_raw[:, 1].rearrange("p j m -> p m j"))
+        interleave(nc.vector.tensor_copy, w_grp[:, 0], w_raw[:, 0])
+        interleave(nc.scalar.copy, w_grp[:, 1], w_raw[:, 1])
         nc.vector.quantize_mx(
             out=w_codes[:].bitcast(FP8X4), scales=w_scales[:], in_=w_grp[:].rearrange("p c m j -> p (c m j)")
         )
@@ -77,12 +84,16 @@ def tile_picked_agg_lin_bias_sub_l_kernel(
             bank = psum.tile([P, n], F32, name=f"y{t0}")
             banks[t0] = bank
 
-        for c, t0, n in LOADS:
-            raw = raws[(c, t0)]
+        def copies(c, t0, n, share):
+            raw = [r[:, :, t0 - s : t0 - s + n] for (q, s, m, r) in raws if q == c and s <= t0 < s + m][0]
             grp = keep.tile([P, n, PACK], BF16, name=f"grp{c}_{t0}", align_bytes=64)
-            cut = n * 5 // 8
-            nc.scalar.copy(out=grp[:, cut:], in_=raw[:, :, cut:].rearrange("p j w -> p w j"))
-            nc.vector.tensor_copy(out=grp[:, :cut], in_=raw[:, :, :cut].rearrange("p j w -> p w j"))
+            cut = n * share // 16
+            if cut < n:
+                interleave(nc.scalar.copy, grp[:, cut:], raw[:, :, cut:])
+            interleave(nc.vector.tensor_copy, grp[:, :cut], raw[:, :, :cut])
+            return grp
+
+        def product(c, t0, n, grp):
             nc.vector.quantize_mx(
                 out=x_codes[:, c, t0 : t0 + n].bitcast(FP8X4),
                 scales=x_scales[:, c, t0 : t0 + n],
@@ -99,12 +110,20 @@ def tile_picked_agg_lin_bias_sub_l_kernel(
                         start=(c == 0),
                         stop=(c == PASSES - 1),
                     )
-                    if c == PASSES - 1:
-                        nc.scalar.activation(
-                            out=y[:, r0 : r0 + rn], in_=banks[r0][:], func=IDENTITY, bias=bias[:]
-                        )
 
-        H = V // 2
+        for c, t0, n, share in UNITS[:2]:
+            grp = copies(c, t0, n, share)
+            product(c, t0, n, grp)
+        grp2 = copies(*UNITS[2])
+        grp3 = copies(*UNITS[3])
+        product(*UNITS[2][:3], grp2)
+        product(*UNITS[3][:3], grp3)
+        grp4 = copies(*UNITS[4])
+        product(*UNITS[4][:3], grp4)
+        nc.scalar.activation(out=y[:, :512], in_=banks[0][:], func=IDENTITY, bias=bias[:])
+        for t0, n in RANGES[1:]:
+            nc.vector.tensor_scalar(out=y[:, t0 : t0 + n], in0=banks[t0][:], scalar1=bias[:], scalar2=None, op0=ADD)
+
         prods = []
         accs = []
         for d in range(D):
@@ -113,7 +132,7 @@ def tile_picked_agg_lin_bias_sub_l_kernel(
         for i in range(V // P):
             acc = psum.tile([P, P], F32, name=f"acc{i}")
             accs.append(acc)
-        back = [psum.tile([P, H], F32, name=f"back{h}", tag=("back0", "y0")[h]) for h in range(2)]
+        backs = [psum.tile([P, 2 * P], F32, name=f"back{h}", tag=("y0", "y512")[h]) for h in range(2)]
         turned = keep.tile([P, V], F32, name="turned")
         res = keep.tile([P, V], F32, name="res")
 
@@ -122,32 +141,28 @@ def tile_picked_agg_lin_bias_sub_l_kernel(
                 prods[d][:, lo:hi], y[:].indirect(offs[d][:, lo // 16 : hi // 16]), gates[d][:, lo:hi], MULT
             )
 
-        def add_up(d, lo, hi, last):
-            for i in range(lo // P, hi // P):
-                nc.tensor.matmul(
-                    accs[i][:], prods[d][:, i * P : (i + 1) * P], ident[:], start=(d == 0), stop=(d == last), is_transpose=True
-                )
+        def add_up(d, i, last):
+            nc.tensor.matmul(
+                accs[i][:], prods[d][:, i * P : (i + 1) * P], ident[:], start=(d == 0), stop=(d == last), is_transpose=True
+            )
 
-        def turn_back(h):
-            for i in range(2 * h, 2 * h + 2):
-                nc.scalar.copy(out=turned[:, i * P : (i + 1) * P], in_=accs[i][:])
-                nc.tensor.transpose(back[h][:, (i - 2 * h) * P : (i - 2 * h + 1) * P], turned[:, i * P : (i + 1) * P], ident[:])
+        def turn_back(i, target):
+            cols = slice(i * P, (i + 1) * P)
+            nc.scalar.copy(out=turned[:, cols], in_=accs[i][:])
+            nc.tensor.transpose(target, turned[:, cols], ident[:])
 
-        for d in range(6):
+        for d in range(D - 2):
             gather(d, 0, V)
-            add_up(d, 0, H, 7)
-            add_up(d, H, V, 5)
-        gather(6, 0, H)
-        add_up(6, 0, H, 7)
-        gather(7, 0, H)
-        turn_back(1)
-        add_up(7, 0, H, 7)
-        gather(6, H, V)
-        gather(7, H, V)
-        turn_back(0)
-        nc.scalar.copy(out=res[:, :H], in_=back[0][:])
-        nc.sync.dma_start(out=out[:, :H], in_=res[:, :H])
-        pair = keep.tile([P, H], F32, name="pair")
-        nc.vector.tensor_tensor(pair[:], prods[6][:, H:], prods[7][:, H:], ADD)
-        nc.vector.tensor_tensor(res[:, H:], pair[:], back[1][:], ADD)
-        nc.sync.dma_start(out=out[:, H:], in_=res[:, H:])
+            for i in range(4):
+                add_up(d, i, D - 2)
+        for h in range(2):
+            gather(D - 2, 2 * h * P, 2 * (h + 1) * P)
+            for i in (2 * h, 2 * h + 1):
+                add_up(D - 2, i, D - 2)
+                turn_back(i, backs[h][:, (i - 2 * h) * P : (i - 2 * h + 1) * P])
+        for h in range(2):
+            gather(D - 1, 2 * h * P, 2 * (h + 1) * P)
+        for h in range(2):
+            lo, hi = 2 * h * P, 2 * (h + 1) * P
+            nc.vector.tensor_tensor(res[:, lo:hi], prods[7][:, lo:hi], backs[h][:], ADD)
+            nc.sync.dma_start(out=out[:, lo:hi], in_=res[:, lo:hi])

@@ -22,9 +22,9 @@ ADD = mybir.AluOpType.add
 IDENTITY = mybir.ActivationFunctionType.Identity
 
 
-LOADS = ((0, 0, 512), (0, 512, 512), (1, 0, 512), (1, 512, 256), (1, 768, 256))
+LOADS = ((0, 0, 1024), (1, 0, 512), (1, 512, 256), (1, 768, 256))
 RANGES = ((0, 512), (512, 256), (768, 256))
-UNITS = ((0, 0, 512, 8), (0, 512, 512, 8), (1, 0, 512, 8), (1, 512, 256, 8), (1, 768, 256, 12))
+UNITS = ((0, 0, 512, 8), (0, 512, 512, 8), (1, 0, 512, 9), (1, 512, 256, 10), (1, 768, 256, 12))
 
 
 def tile_picked_agg_lin_bias_sub_l_kernel(
@@ -36,6 +36,8 @@ def tile_picked_agg_lin_bias_sub_l_kernel(
         keep = ctx.enter_context(tc.tile_pool(name="keep", bufs=1))
         psum = ctx.enter_context(tc.psum_pool(name="psum", bufs=1))
 
+        bias = keep.tile([P, 1], F32, name="bias")
+        nc.scalar.dma_start(out=bias[:], in_=b)
         ident = keep.tile([P, P], F32, name="ident")
         make_identity(nc, ident[:])
 
@@ -49,8 +51,6 @@ def tile_picked_agg_lin_bias_sub_l_kernel(
                 in_=xT[c * K_PASS : (c + 1) * K_PASS, t0 : t0 + n].rearrange("(p j) w -> p j w", j=PACK),
             )
             raws.append((c, t0, n, raw))
-        bias = keep.tile([P, 1], F32, name="bias")
-        nc.sync.dma_start(out=bias[:], in_=b)
         offs = []
         gates = []
         for d in range(D):
@@ -146,11 +146,6 @@ def tile_picked_agg_lin_bias_sub_l_kernel(
                 accs[i][:], prods[d][:, i * P : (i + 1) * P], ident[:], start=(d == 0), stop=(d == last), is_transpose=True
             )
 
-        def turn_back(i, target):
-            cols = slice(i * P, (i + 1) * P)
-            nc.scalar.copy(out=turned[:, cols], in_=accs[i][:])
-            nc.tensor.transpose(target, turned[:, cols], ident[:])
-
         for d in range(D - 2):
             gather(d, 0, V)
             for i in range(4):
@@ -159,7 +154,10 @@ def tile_picked_agg_lin_bias_sub_l_kernel(
             gather(D - 2, 2 * h * P, 2 * (h + 1) * P)
             for i in (2 * h, 2 * h + 1):
                 add_up(D - 2, i, D - 2)
-                turn_back(i, backs[h][:, (i - 2 * h) * P : (i - 2 * h + 1) * P])
+        for i in range(4):
+            nc.scalar.copy(out=turned[:, i * P : (i + 1) * P], in_=accs[i][:])
+        for i in range(4):
+            nc.tensor.transpose(backs[i // 2][:, i % 2 * P : (i % 2 + 1) * P], turned[:, i * P : (i + 1) * P], ident[:])
         for h in range(2):
             gather(D - 1, 2 * h * P, 2 * (h + 1) * P)
         for h in range(2):

@@ -23,8 +23,9 @@ IDENTITY = mybir.ActivationFunctionType.Identity
 
 
 LOADS = ((0, 0, 1024), (1, 0, 512), (1, 512, 256), (1, 768, 256))
-RANGES = ((0, 512), (512, 256), (768, 256))
-UNITS = ((0, 0, 512, 8), (0, 512, 512, 8), (1, 0, 512, 9), (1, 512, 256, 10), (1, 768, 256, 12))
+RANGES = ((0, 512), (512, 256), (768, 128), (896, 128))
+UNITS = ((0, 0, 512, 8), (0, 512, 512, 8), (1, 0, 512, 9), (1, 512, 256, 11))
+LAST = ((1, 768, 128, 16), (1, 896, 128, 16))
 
 
 def tile_picked_agg_lin_bias_sub_l_kernel(
@@ -111,18 +112,20 @@ def tile_picked_agg_lin_bias_sub_l_kernel(
                         stop=(c == PASSES - 1),
                     )
 
-        for c, t0, n, share in UNITS[:2]:
+        def bring(t0, n):
+            nc.scalar.activation(out=y[:, t0 : t0 + n], in_=banks[t0][:], func=IDENTITY, bias=bias[:])
+
+        for c, t0, n, share in UNITS:
             grp = copies(c, t0, n, share)
             product(c, t0, n, grp)
-        grp2 = copies(*UNITS[2])
-        grp3 = copies(*UNITS[3])
-        product(*UNITS[2][:3], grp2)
-        product(*UNITS[3][:3], grp3)
-        grp4 = copies(*UNITS[4])
-        product(*UNITS[4][:3], grp4)
-        nc.scalar.activation(out=y[:, :512], in_=banks[0][:], func=IDENTITY, bias=bias[:])
-        for t0, n in RANGES[1:]:
-            nc.vector.tensor_scalar(out=y[:, t0 : t0 + n], in0=banks[t0][:], scalar1=bias[:], scalar2=None, op0=ADD)
+        grps = [copies(*unit) for unit in LAST]
+        for t0, n in RANGES[:2]:
+            bring(t0, n)
+        for (c, t0, n, share), grp in zip(LAST, grps):
+            product(c, t0, n, grp)
+        bring(*RANGES[2])
+        t0, n = RANGES[3]
+        nc.vector.tensor_scalar(out=y[:, t0 : t0 + n], in0=banks[t0][:], scalar1=bias[:], scalar2=None, op0=ADD)
 
         prods = []
         accs = []

from contextlib import ExitStack

import concourse.mybir as mybir
from concourse.masks import make_identity

K, T, D, V, M = 1024, 1024, 8, 512, 128
P = 128
PACK = 4
K_PASS = P * PACK
PASSES = K // K_PASS

FLOPS = 2 * K * T * M + 2 * D * V * M

F32 = mybir.dt.float32
BF16 = mybir.dt.bfloat16
U32 = mybir.dt.uint32
U16 = mybir.dt.uint16
U8 = mybir.dt.uint8
FP8X4 = mybir.dt.float8_e4m3fn_x4
MULT = mybir.AluOpType.mult
ADD = mybir.AluOpType.add
IDENTITY = mybir.ActivationFunctionType.Identity


LOADS = ((0, 0, 1024), (1, 0, 512), (1, 512, 256), (1, 768, 256))
RANGES = ((0, 512), (512, 256), (768, 128), (896, 128))
UNITS = ((0, 0, 512, 8), (0, 512, 512, 8), (1, 0, 512, 9), (1, 512, 256, 11))
LAST = ((1, 768, 128, 16), (1, 896, 128, 16))


def tile_picked_agg_lin_bias_sub_l_kernel(
    tc, xT, w, b, gate, pos1, pos2, pos3, pos4, pos5, pos6, pos7, pos8, out
):
    nc = tc.nc
    lists = (pos1, pos2, pos3, pos4, pos5, pos6, pos7, pos8)
    with ExitStack() as ctx:
        keep = ctx.enter_context(tc.tile_pool(name="keep", bufs=1))
        psum = ctx.enter_context(tc.psum_pool(name="psum", bufs=1))

        bias = keep.tile([P, 1], F32, name="bias")
        nc.scalar.dma_start(out=bias[:], in_=b)
        ident = keep.tile([P, P], F32, name="ident")
        make_identity(nc, ident[:])

        w_raw = keep.tile([P, PASSES, PACK, M], F32, name="w_raw")
        nc.sync.dma_start(out=w_raw[:], in_=w.rearrange("(c p j) m -> p c j m", c=PASSES, j=PACK))
        raws = []
        for c, t0, n in LOADS:
            raw = keep.tile([P, PACK, n], F32, name=f"raw{c}_{t0}")
            nc.sync.dma_start(
                out=raw[:],
                in_=xT[c * K_PASS : (c + 1) * K_PASS, t0 : t0 + n].rearrange("(p j) w -> p j w", j=PACK),
            )
            raws.append((c, t0, n, raw))
        offs = []
        gates = []
        for d in range(D):
            off = keep.tile([P, V // 16], U16, name=f"off{d}")
            nc.sync.dma_start(off[:], lists[d])
            offs.append(off)
            g = keep.tile([P, V], F32, name=f"gate{d}")
            nc.sync.dma_start(out=g[:], in_=gate[d])
            gates.append(g)

        def interleave(copy, grouped, raw):
            copy(
                out=grouped.rearrange("p (g i) j -> p g j i", i=4),
                in_=raw.rearrange("p j (g i) -> p g j i", i=4),
            )

        w_grp = keep.tile([P, PASSES, M, PACK], BF16, name="w_grp", align_bytes=64)
        w_codes = keep.tile([P, PASSES * M], U32, name="w_codes", align_bytes=64)
        w_scales = keep.tile([P, PASSES * M], U8, name="w_scales", align_bytes=64)
        interleave(nc.vector.tensor_copy, w_grp[:, 0], w_raw[:, 0])
        interleave(nc.scalar.copy, w_grp[:, 1], w_raw[:, 1])
        nc.vector.quantize_mx(
            out=w_codes[:].bitcast(FP8X4), scales=w_scales[:], in_=w_grp[:].rearrange("p c m j -> p (c m j)")
        )

        y = keep.tile([P, T], F32, name="y")
        x_codes = keep.tile([P, PASSES, T], U32, name="x_codes", align_bytes=64)
        x_scales = keep.tile([P, PASSES, T], U8, name="x_scales", align_bytes=64)
        banks = {}
        for t0, n in RANGES:
            bank = psum.tile([P, n], F32, name=f"y{t0}")
            banks[t0] = bank

        def copies(c, t0, n, share):
            raw = [r[:, :, t0 - s : t0 - s + n] for (q, s, m, r) in raws if q == c and s <= t0 < s + m][0]
            grp = keep.tile([P, n, PACK], BF16, name=f"grp{c}_{t0}", align_bytes=64)
            cut = n * share // 16
            if cut < n:
                interleave(nc.scalar.copy, grp[:, cut:], raw[:, :, cut:])
            interleave(nc.vector.tensor_copy, grp[:, :cut], raw[:, :, :cut])
            return grp

        def product(c, t0, n, grp):
            nc.vector.quantize_mx(
                out=x_codes[:, c, t0 : t0 + n].bitcast(FP8X4),
                scales=x_scales[:, c, t0 : t0 + n],
                in_=grp[:].rearrange("p w j -> p (w j)"),
            )
            for r0, rn in RANGES:
                if t0 <= r0 < t0 + n:
                    nc.tensor.matmul_mx(
                        out=banks[r0][:],
                        lhsT=w_codes[:, c * M : (c + 1) * M].bitcast(FP8X4),
                        lhsT_scale=w_scales[:, c * M : (c + 1) * M],
                        rhs=x_codes[:, c, r0 : r0 + rn].bitcast(FP8X4),
                        rhs_scale=x_scales[:, c, r0 : r0 + rn],
                        start=(c == 0),
                        stop=(c == PASSES - 1),
                    )

        def bring(t0, n):
            nc.scalar.activation(out=y[:, t0 : t0 + n], in_=banks[t0][:], func=IDENTITY, bias=bias[:])

        for c, t0, n, share in UNITS:
            grp = copies(c, t0, n, share)
            product(c, t0, n, grp)
        grps = [copies(*unit) for unit in LAST]
        for t0, n in RANGES[:2]:
            bring(t0, n)
        for (c, t0, n, share), grp in zip(LAST, grps):
            product(c, t0, n, grp)
        bring(*RANGES[2])
        t0, n = RANGES[3]
        nc.vector.tensor_scalar(out=y[:, t0 : t0 + n], in0=banks[t0][:], scalar1=bias[:], scalar2=None, op0=ADD)

        prods = []
        accs = []
        for d in range(D):
            prod = keep.tile([P, V], F32, name=f"prod{d}")
            prods.append(prod)
        for i in range(V // P):
            acc = psum.tile([P, P], F32, name=f"acc{i}")
            accs.append(acc)
        backs = [psum.tile([P, 2 * P], F32, name=f"back{h}", tag=("y0", "y512")[h]) for h in range(2)]
        turned = keep.tile([P, V], F32, name="turned")
        res = keep.tile([P, V], F32, name="res")

        def gather(d, lo, hi):
            nc.vector.tensor_tensor(
                prods[d][:, lo:hi], y[:].indirect(offs[d][:, lo // 16 : hi // 16]), gates[d][:, lo:hi], MULT
            )

        def add_up(d, i, last):
            nc.tensor.matmul(
                accs[i][:], prods[d][:, i * P : (i + 1) * P], ident[:], start=(d == 0), stop=(d == last), is_transpose=True
            )

        for d in range(D - 2):
            gather(d, 0, V)
            for i in range(4):
                add_up(d, i, D - 2)
        for h in range(2):
            gather(D - 2, 2 * h * P, 2 * (h + 1) * P)
            for i in (2 * h, 2 * h + 1):
                add_up(D - 2, i, D - 2)
        for i in range(4):
            nc.scalar.copy(out=turned[:, i * P : (i + 1) * P], in_=accs[i][:])
        for i in range(4):
            nc.tensor.transpose(backs[i // 2][:, i % 2 * P : (i % 2 + 1) * P], turned[:, i * P : (i + 1) * P], ident[:])
        for h in range(2):
            gather(D - 1, 2 * h * P, 2 * (h + 1) * P)
        for h in range(2):
            lo, hi = 2 * h * P, 2 * (h + 1) * P
            nc.vector.tensor_tensor(res[:, lo:hi], prods[7][:, lo:hi], backs[h][:], ADD)
            nc.sync.dma_start(out=out[:, lo:hi], in_=res[:, lo:hi])
